import numpy as np
import ml_dtypes


def mxq(x, axis, fmt="e4m3"):
    dtype, down = {"e4m3": (ml_dtypes.float8_e4m3fn, 7), "e5m2": (ml_dtypes.float8_e5m2, 14)}[fmt]
    v = np.moveaxis(np.asarray(x, np.float32).astype(ml_dtypes.bfloat16).astype(np.float64), axis, -1)
    blocks = v.reshape(v.shape[:-1] + (-1, 32))
    amax = np.abs(blocks).max(-1, keepdims=True)
    byte = np.maximum(np.where(amax > 0, np.frexp(amax)[1] - 1 + 127, 0) - down, 1)
    scale = np.exp2(byte - 127.0)
    codes = (blocks / scale).astype(np.float32).astype(dtype).astype(np.float64)
    return np.moveaxis((codes * scale).reshape(v.shape), -1, axis)


WIDE = False


def mx_kscale(k, group=512):
    if not WIDE:
        return np.ones(k)
    levels = np.array([10, -10, 5, -5, 0])
    if group != 512:
        return np.exp2(np.random.permutation(np.resize(levels, k // group))).repeat(group)
    if k % 512:
        return np.exp2(np.random.permutation(np.resize(levels, k // 32))).repeat(32)
    a = np.empty((k // 512, 16))
    for p in range(k // 512):
        a[p, :8] = np.random.permutation(np.resize(levels, 8))
        for g in range(8):
            far = levels[np.abs(levels - a[p, g]) >= 10]
            a[p, g + 8] = far[np.random.randint(len(far))]
    return np.exp2(a.ravel()).repeat(32)


def f64(x):
    return np.asarray(x).astype(np.float64)


def striped(idx):
    return np.tile(np.asarray(idx).reshape(-1, 16).T, (8, 1)).astype(np.uint16)


def unstriped(offs):
    return offs[:16].T.reshape(-1).astype(np.int64)


H, KV, D, NQ, N = 4, 4, 128, 512, 512


def setup_inputs():
    n = np.random.standard_normal
    s = mx_kscale(D, 0)[:, None]
    u = mx_kscale(N)
    t = np.random.uniform(0.5, 2.0, N) * u
    v = n((KV, N, 128))
    return {
        "qT": (n((H, D, NQ)) * s * (0.70 / np.sqrt(D))).astype(np.float32),
        "kT": (n((KV, D, N)) / s).astype(np.float32),
        "t": t.reshape(N, 1).astype(np.float32),
        "v": (v / t[:, None]).astype(np.float32),
        "kb": (0.5 * n((N, 1))).astype(np.float32),
    }


def reference(qT, kT, t, v, kb):
    a = mxq(f64(kT), 1, "e4m3").transpose(0, 2, 1) @ mxq(f64(qT), 1, "e4m3")
    a = a + f64(kb)
    p = 1.0 / (1.0 + np.exp(-a))
    w = p * f64(t)
    y = mxq(w, 1, "e4m3").transpose(0, 2, 1) @ mxq(f64(v), 1, "e4m3")
    y = y / 16.0
    return y

@@ -1,0 +1,233 @@
+from contextlib import ExitStack
+
+import concourse.mybir as mybir
+
+H, D, NQ, NT, E = 4, 128, 512, 512, 128
+FLOPS = 2 * H * NT * NQ * D + 2 * H * NQ * NT * E
+
+F32 = mybir.dt.float32
+BF16 = mybir.dt.bfloat16
+U32 = mybir.dt.uint32
+U8 = mybir.dt.uint8
+FP8X4 = mybir.dt.float8_e4m3fn_x4
+ACT = mybir.ActivationFunctionType
+ALU = mybir.AluOpType
+
+P = 128
+PACK = 4
+ROWS = 32
+QT = 128
+UNITS = H * NQ // QT
+
+
+def tile_rows_sigmoid_kb_kernel(tc, qT, kT, t, v, kb, out):
+    nc = tc.nc
+    with ExitStack() as ctx:
+        sb = ctx.enter_context(tc.tile_pool(name="sb", bufs=1))
+        ps = ctx.enter_context(tc.psum_pool(name="ps", bufs=1))
+        ctx.enter_context(tc.manual_schedule())
+
+        def sbuf(name, shape, dtype):
+            return sb.tile(shape, dtype, name=name, align_bytes=64)
+
+        q_hbm = qT.rearrange("h (p j) n -> (h p) j n", j=PACK)
+        k_hbm = kT.rearrange("h (p j) n -> (h p) j n", j=PACK)
+
+        t_sb = sbuf("t_sb", [P, PACK], F32)
+        kb_sb = sbuf("kb_sb", [P, PACK], F32)
+        warm_in = sbuf("warm_in", [P, 1], F32)
+        warm_out = sbuf("warm_out", [P, 1], F32)
+        k_raw = [sbuf("k_raw%d" % a, [P, PACK, NT // 2], F32) for a in range(2)]
+        q_spans = [(0, 128), (128, 256), (256, 512)]
+        q_raw = [sbuf("q_raw%d" % a, [P, PACK, hi - lo], F32) for a, (lo, hi) in enumerate(q_spans)]
+        v_raw = [sbuf("v_raw%d" % a, [P, 2, PACK, E], F32) for a in range(2)]
+
+        k_bf = [sbuf("k_bf%d" % u, [P, 2, P, PACK], BF16) for u in range(2)]
+        k_codes = [sbuf("k_codes%d" % u, [P, 2 * P], U32) for u in range(2)]
+        k_scales = [sbuf("k_scales%d" % u, [P, 2 * P], U8) for u in range(2)]
+        q_bf = [sbuf("q_bf%d" % a, [P, hi - lo, PACK], BF16) for a, (lo, hi) in enumerate(q_spans)]
+        q_codes = [sbuf("q_codes%d" % a, [P, hi - lo], U32) for a, (lo, hi) in enumerate(q_spans)]
+        q_scales = [sbuf("q_scales%d" % a, [P, hi - lo], U8) for a, (lo, hi) in enumerate(q_spans)]
+        v_bf = [sbuf("v_bf%d" % a, [P, 2, E, PACK], BF16) for a in range(2)]
+        v_codes = [sbuf("v_codes%d" % a, [P, 2 * E], U32) for a in range(2)]
+        v_scales = [sbuf("v_scales%d" % a, [P, 2 * E], U8) for a in range(2)]
+        p_sb = [sbuf("p_sb%d" % u, [P, PACK, QT], F32) for u in range(UNITS)]
+        w_bf = [sbuf("w_bf%d" % u, [P, QT, PACK], BF16) for u in range(UNITS)]
+        w_codes = [sbuf("w_codes%d" % u, [P, QT], U32) for u in range(UNITS)]
+        w_scales = [sbuf("w_scales%d" % u, [P, QT], U8) for u in range(UNITS)]
+        score = [ps.tile([P, PACK, QT], F32, name="score%d" % h) for h in range(H)]
+        y_bank = [ps.tile([P, H, E], F32, name="y_bank%d" % g) for g in range(4)]
+
+        def quantize(codes, scales, src):
+            nc.vector.quantize_mx(out=codes[:].bitcast(FP8X4), scales=scales[:], in_=src)
+
+        def cast(eng, dst, src):
+            if eng == "v":
+                nc.vector.tensor_copy(out=dst, in_=src)
+            else:
+                nc.scalar.copy(out=dst, in_=src)
+
+        def cast_k(eng, a, u):
+            dst = k_bf[u][:, :, 64 * a : 64 * a + 64, :].rearrange("p r s j -> p s j r")
+            src = k_raw[a][:].rearrange("p j (s r) -> p s j r", r=PACK)[:, :, :, 2 * u : 2 * u + 2]
+            cast(eng, dst, src)
+
+        def cast_pairs(eng, dst, src):
+            cast(eng, dst.rearrange("p (c i) j -> p c j i", i=2), src.rearrange("p j (c i) -> p c j i", i=2))
+
+        def quant_k(u):
+            quantize(k_codes[u], k_scales[u], k_bf[u][:].rearrange("p r s j -> p (r s j)"))
+
+        def quant_q(a):
+            quantize(q_codes[a], q_scales[a], q_bf[a][:].rearrange("p n j -> p (n j)"))
+
+        def cast_v(eng, h):
+            cast_pairs(eng, v_bf[h // 2][:, h % 2, :, :], v_raw[h // 2][:, h % 2, :, :])
+
+        def quant_v(a):
+            quantize(v_codes[a], v_scales[a], v_bf[a][:].rearrange("p h e r -> p (h e r)"))
+
+        def scores(units):
+            for r in range(PACK):
+                for u in units:
+                    h, qc = u % H, u // H
+                    a = min(qc, 2)
+                    rows = slice(ROWS * h, ROWS * h + ROWS)
+                    kc = slice(P * (r % 2), P * (r % 2) + P)
+                    qcols = slice(QT * qc - q_spans[a][0], QT * qc - q_spans[a][0] + QT)
+                    nc.tensor.matmul_mx(
+                        out=score[h][:, r, :],
+                        lhsT=k_codes[r // 2][rows, kc].bitcast(FP8X4),
+                        lhsT_scale=k_scales[r // 2][rows, kc],
+                        rhs=q_codes[a][rows, qcols].bitcast(FP8X4),
+                        rhs_scale=q_scales[a][rows, qcols],
+                        start=True,
+                        stop=True,
+                    )
+
+        def sigmoid(u):
+            for r in range(PACK):
+                nc.scalar.activation(
+                    out=p_sb[u][:, r, :], in_=score[u % H][:, r, :], func=ACT.Sigmoid, bias=kb_sb[:, r : r + 1]
+                )
+
+        def weigh(u):
+            nc.vector.tensor_tensor(
+                out=w_bf[u][:].rearrange("p (c i) r -> p c r i", i=2),
+                in0=p_sb[u][:].rearrange("p r (c i) -> p c r i", i=2),
+                in1=t_sb[:].rearrange("p (c r i) -> p c r i", c=1, i=1).to_broadcast([P, QT // 2, PACK, 2]),
+                op=ALU.mult,
+            )
+
+        def quant_w(u):
+            quantize(w_codes[u], w_scales[u], w_bf[u][:].rearrange("p n r -> p (n r)"))
+
+        def y_place(u):
+            if u < 14:
+                return u // H, u % H
+            return u - 14, 0
+
+        def product(u):
+            h = u % H
+            g, place = y_place(u)
+            ec = slice(E * (h % 2), E * (h % 2) + E)
+            nc.tensor.matmul_mx(
+                out=y_bank[g][:, place, :],
+                lhsT=w_codes[u][:].bitcast(FP8X4),
+                lhsT_scale=w_scales[u][:],
+                rhs=v_codes[h // 2][:, ec].bitcast(FP8X4),
+                rhs_scale=v_scales[h // 2][:, ec],
+                start=True,
+                stop=True,
+            )
+
+        def emit(u0, n):
+            g, place = y_place(u0)
+            h, qc = u0 % H, u0 // H
+            y_sb = sbuf("y_sb%d" % u0, [P, n, E], F32)
+            nc.scalar.activation(out=y_sb[:], in_=y_bank[g][:, place : place + n, :], func=ACT.Copy, scale=1.0 / 16.0)
+            nc.sync.dma_start(
+                out=out[h : h + n, QT * qc : QT * qc + QT, :].rearrange("h p e -> p h e"), in_=y_sb[:]
+            )
+
+        nc.scalar.dma_start(out=kb_sb[:], in_=kb.rearrange("(p r) o -> p (r o)", r=PACK))
+        nc.scalar.dma_start(out=t_sb[:], in_=t.rearrange("(p r) o -> p (r o)", r=PACK))
+        for a in range(2):
+            nc.sync.dma_start(out=k_raw[a][:], in_=k_hbm[:, :, 256 * a : 256 * a + 256])
+        for a, (lo, hi) in enumerate(q_spans):
+            nc.sync.dma_start(out=q_raw[a][:], in_=q_hbm[:, :, lo:hi])
+        for a in range(2):
+            nc.sync.dma_start(
+                out=v_raw[a][:].rearrange("p h r e -> p h (r e)"),
+                in_=v[2 * a : 2 * a + 2].rearrange("h (p r) e -> p h (r e)", r=PACK),
+            )
+        nc.gpsimd.memset(warm_in[:], 0.0)
+        nc.scalar.activation(out=warm_out[:], in_=warm_in[:], func=ACT.Sigmoid)
+
+        cast_k("v", 0, 0)
+        cast_k("v", 0, 1)
+        cast_k("v", 1, 0)
+        cast_k("s", 1, 1)
+        quant_k(0)
+        cast_pairs("s", q_bf[0][:, 0:48, :], q_raw[0][:, :, 0:48])
+        cast_pairs("v", q_bf[0][:, 48:128, :], q_raw[0][:, :, 48:128])
+        quant_k(1)
+        quant_q(0)
+        scores([0, 1])
+        scores([2, 3])
+        cast_pairs("v", q_bf[1][:], q_raw[1][:])
+        sigmoid(0)
+        weigh(0)
+        quant_q(1)
+        sigmoid(1)
+        scores([4, 5])
+        quant_w(0)
+        weigh(1)
+        cast_pairs("v", q_bf[2][:], q_raw[2][:])
+        quant_w(1)
+        sigmoid(2)
+        weigh(2)
+        quant_q(2)
+        sigmoid(3)
+        scores([6, 7])
+        weigh(3)
+        quant_w(2)
+        cast_v("s", 0)
+        sigmoid(4)
+        cast_v("v", 2)
+        quant_w(3)
+        cast_v("v", 3)
+        cast_v("s", 1)
+        sigmoid(5)
+        scores([8, 9])
+        weigh(4)
+        quant_v(1)
+        quant_v(0)
+        for u in range(5, UNITS):
+            if u > 5:
+                sigmoid(u)
+            if u % 2 == 1 and 5 < u < 12:
+                scores([u + 3, u + 4])
+            if u == 7:
+                for w in range(0, 4):
+                    product(w)
+            if u == 10:
+                emit(0, 4)
+            if u == 11:
+                for w in range(4, 8):
+                    product(w)
+            if u == 14:
+                emit(4, 4)
+            weigh(u)
+            quant_w(u - 1)
+            if u >= 12:
+                product(u - 4)
+        quant_w(UNITS - 1)
+        emit(8, 4)
+        product(12)
+        product(13)
+        product(14)
+        product(15)
+        emit(12, 2)
+        emit(14, 1)
+        emit(15, 1)

@@ -51,12 +51,55 @@ def tile_rows_sigmoid_kb_kernel(tc, qT, kT, t, v, kb, out):
         v_bf = [sbuf("v_bf%d" % a, [P, 2, E, PACK], BF16) for a in range(2)]
         v_codes = [sbuf("v_codes%d" % a, [P, 2 * E], U32) for a in range(2)]
         v_scales = [sbuf("v_scales%d" % a, [P, 2 * E], U8) for a in range(2)]
-        p_sb = [sbuf("p_sb%d" % u, [P, PACK, QT], F32) for u in range(UNITS)]
+        p_wide = [sbuf("p_sbw%d" % h, [P, PACK, 2 * QT], F32) for h in range(H)]
+        p_sb = [sbuf("p_sb%d" % u, [P, PACK, QT], F32)[:] for u in range(8)]
+        p_sb.extend([p_wide[u // 2][:, :, QT * (u % 2) : QT * (u % 2) + QT] for u in range(8)])
         w_bf = [sbuf("w_bf%d" % u, [P, QT, PACK], BF16) for u in range(UNITS)]
         w_codes = [sbuf("w_codes%d" % u, [P, QT], U32) for u in range(UNITS)]
         w_scales = [sbuf("w_scales%d" % u, [P, QT], U8) for u in range(UNITS)]
         score = [ps.tile([P, PACK, QT], F32, name="score%d" % h) for h in range(H)]
-        y_bank = [ps.tile([P, H, E], F32, name="y_bank%d" % g) for g in range(4)]
+        spare = {h: ps.tile([P, PACK, QT], F32, name="spare%d" % h) for h in (0, 2)}
+        y_bank = [ps.tile([P, H, E], F32, name="y_bank%d" % g) for g in range(2)]
+
+        def unit(u):
+            if u < 8:
+                return u % H, u // H
+            return (u - 8) // 2, 2 + u % 2
+
+        def score_at(u, r):
+            if u == 0 and r >= 2:
+                return spare[0][:, r, :]
+            return score[u % H][:, r, :]
+
+        def wide_bank(h, half):
+            return spare[h] if h in spare and half == 0 else score[h]
+
+        def scores_wide(fills):
+            for n in range(PACK):
+                for h, half in fills:
+                    rows = slice(ROWS * h, ROWS * h + ROWS)
+                    kc = slice(P * (n // 2), P * (n // 2) + P)
+                    qcols = slice(QT * (n % 2), QT * (n % 2) + QT)
+                    nc.tensor.matmul_mx(
+                        out=wide_bank(h, half)[:, n, :],
+                        lhsT=k_codes[half][rows, kc].bitcast(FP8X4),
+                        lhsT_scale=k_scales[half][rows, kc],
+                        rhs=q_codes[2][rows, qcols].bitcast(FP8X4),
+                        rhs_scale=q_scales[2][rows, qcols],
+                        start=True,
+                        stop=True,
+                    )
+
+        def sigmoid_wide(h, half):
+            for m in range(2):
+                r = 2 * half + m
+                nc.scalar.activation(
+                    out=p_wide[h][:, r, :],
+                    in_=wide_bank(h, half)[:, 2 * m : 2 * m + 2, :].rearrange("p a n -> p (a n)"),
+                    func=ACT.Sigmoid,
+                    bias=kb_sb[:, r : r + 1],
+                )
+
 
         def quantize(codes, scales, src):
             nc.vector.quantize_mx(out=codes[:].bitcast(FP8X4), scales=scales[:], in_=src)
@@ -96,7 +139,7 @@ def tile_rows_sigmoid_kb_kernel(tc, qT, kT, t, v, kb, out):
                     kc = slice(P * (r % 2), P * (r % 2) + P)
                     qcols = slice(QT * qc - q_spans[a][0], QT * qc - q_spans[a][0] + QT)
                     nc.tensor.matmul_mx(
-                        out=score[h][:, r, :],
+                        out=score_at(u, r),
                         lhsT=k_codes[r // 2][rows, kc].bitcast(FP8X4),
                         lhsT_scale=k_scales[r // 2][rows, kc],
                         rhs=q_codes[a][rows, qcols].bitcast(FP8X4),
@@ -108,13 +151,13 @@ def tile_rows_sigmoid_kb_kernel(tc, qT, kT, t, v, kb, out):
         def sigmoid(u):
             for r in range(PACK):
                 nc.scalar.activation(
-                    out=p_sb[u][:, r, :], in_=score[u % H][:, r, :], func=ACT.Sigmoid, bias=kb_sb[:, r : r + 1]
+                    out=p_sb[u][:, r, :], in_=score_at(u, r), func=ACT.Sigmoid, bias=kb_sb[:, r : r + 1]
                 )
 
         def weigh(u):
             nc.vector.tensor_tensor(
                 out=w_bf[u][:].rearrange("p (c i) r -> p c r i", i=2),
-                in0=p_sb[u][:].rearrange("p r (c i) -> p c r i", i=2),
+                in0=p_sb[u].rearrange("p r (c i) -> p c r i", i=2),
                 in1=t_sb[:].rearrange("p (c r i) -> p c r i", c=1, i=1).to_broadcast([P, QT // 2, PACK, 2]),
                 op=ALU.mult,
             )
@@ -124,11 +167,11 @@ def tile_rows_sigmoid_kb_kernel(tc, qT, kT, t, v, kb, out):
 
         def y_place(u):
             if u < 14:
-                return u // H, u % H
-            return u - 14, 0
+                return u // H % 2, u % H
+            return u % 2, 0
 
         def product(u):
-            h = u % H
+            h = unit(u)[0]
             g, place = y_place(u)
             ec = slice(E * (h % 2), E * (h % 2) + E)
             nc.tensor.matmul_mx(
@@ -141,14 +184,24 @@ def tile_rows_sigmoid_kb_kernel(tc, qT, kT, t, v, kb, out):
                 stop=True,
             )
 
-        def emit(u0, n):
+        def emit(u0, n, eng="s"):
             g, place = y_place(u0)
-            h, qc = u0 % H, u0 // H
+            h, qc = unit(u0)
             y_sb = sbuf("y_sb%d" % u0, [P, n, E], F32)
-            nc.scalar.activation(out=y_sb[:], in_=y_bank[g][:, place : place + n, :], func=ACT.Copy, scale=1.0 / 16.0)
-            nc.sync.dma_start(
-                out=out[h : h + n, QT * qc : QT * qc + QT, :].rearrange("h p e -> p h e"), in_=y_sb[:]
-            )
+            if eng == "s":
+                nc.scalar.activation(out=y_sb[:], in_=y_bank[g][:, place : place + n, :], func=ACT.Copy, scale=1.0 / 16.0)
+            else:
+                nc.vector.tensor_scalar(out=y_sb[:], in0=y_bank[g][:, place : place + n, :], scalar1=1.0 / 16.0, scalar2=None, op0=ALU.mult)
+            if u0 < 8:
+                dst = out[h : h + n, QT * qc : QT * qc + QT, :].rearrange("h p e -> p h e")
+                nc.sync.dma_start(out=dst, in_=y_sb[:])
+            elif n == 4:
+                for a in range(2):
+                    dst = out[h + a, QT * qc : QT * (qc + 2), :].rearrange("(c p) e -> p c e", p=P)
+                    nc.sync.dma_start(out=dst, in_=y_sb[:, 2 * a : 2 * a + 2, :])
+            else:
+                dst = out[h, QT * qc : QT * (qc + n), :].rearrange("(c p) e -> p c e", p=P)
+                nc.sync.dma_start(out=dst, in_=y_sb[:])
 
         nc.scalar.dma_start(out=kb_sb[:], in_=kb.rearrange("(p r) o -> p (r o)", r=PACK))
         nc.scalar.dma_start(out=t_sb[:], in_=t.rearrange("(p r) o -> p (r o)", r=PACK))
@@ -173,61 +226,93 @@ def tile_rows_sigmoid_kb_kernel(tc, qT, kT, t, v, kb, out):
         cast_pairs("v", q_bf[0][:, 48:128, :], q_raw[0][:, :, 48:128])
         quant_k(1)
         quant_q(0)
-        scores([0, 1])
-        scores([2, 3])
-        cast_pairs("v", q_bf[1][:], q_raw[1][:])
+        scores([0])
+        scores([1, 2])
+        scores([3])
+        cast_pairs("s", q_bf[1][:], q_raw[1][:])
+        quant_q(1)
+        cast_pairs("v", q_bf[2][:], q_raw[2][:])
         sigmoid(0)
         weigh(0)
-        quant_q(1)
+        quant_q(2)
         sigmoid(1)
-        scores([4, 5])
-        quant_w(0)
+        scores([4,5])
         weigh(1)
-        cast_pairs("v", q_bf[2][:], q_raw[2][:])
-        quant_w(1)
+        quant_w(0)
         sigmoid(2)
         weigh(2)
-        quant_q(2)
+        quant_w(1)
         sigmoid(3)
-        scores([6, 7])
+        scores([6,7])
+        scores_wide([(0,0),(2,0)])
+        cast_v("v",0)
         weigh(3)
         quant_w(2)
-        cast_v("s", 0)
         sigmoid(4)
-        cast_v("v", 2)
-        quant_w(3)
-        cast_v("v", 3)
-        cast_v("s", 1)
-        sigmoid(5)
-        scores([8, 9])
+        cast_v("s",1)
         weigh(4)
-        quant_v(1)
+        quant_w(3)
+        cast_v("v",2)
+        sigmoid(5)
+        scores_wide([(1,0),(0,1)])
+        weigh(5)
+        quant_w(4)
         quant_v(0)
-        for u in range(5, UNITS):
-            if u > 5:
-                sigmoid(u)
-            if u % 2 == 1 and 5 < u < 12:
-                scores([u + 3, u + 4])
-            if u == 7:
-                for w in range(0, 4):
-                    product(w)
-            if u == 10:
-                emit(0, 4)
-            if u == 11:
-                for w in range(4, 8):
-                    product(w)
-            if u == 14:
-                emit(4, 4)
-            weigh(u)
-            quant_w(u - 1)
-            if u >= 12:
-                product(u - 4)
-        quant_w(UNITS - 1)
-        emit(8, 4)
+        sigmoid(6)
+        cast_v("v",3)
+        weigh(6)
+        quant_w(5)
+        sigmoid(7)
+        scores_wide([(3,0),(2,1)])
+        weigh(7)
+        quant_w(6)
+        quant_v(1)
+        sigmoid_wide(0,0)
+        sigmoid_wide(1,0)
+        scores_wide([(1,1)])
+        sigmoid_wide(0,1)
+        weigh(8)
+        quant_w(7)
+        weigh(9)
+        quant_w(8)
+        sigmoid_wide(3,0)
+        scores_wide([(3,1)])
+        product(0)
+        product(1)
+        product(2)
+        product(3)
+        product(4)
+        product(5)
+        product(6)
+        product(7)
+        sigmoid_wide(1,1)
+        weigh(10)
+        quant_w(9)
+        weigh(11)
+        quant_w(10)
+        sigmoid_wide(2,0)
+        sigmoid_wide(2,1)
+        emit(0,4)
+        product(8)
+        product(9)
+        product(10)
+        weigh(12)
+        quant_w(11)
+        product(11)
+        sigmoid_wide(3,1)
+        emit(4,4)
+        weigh(13)
+        quant_w(12)
         product(12)
+        emit(8,4)
+        weigh(14)
+        quant_w(13)
         product(13)
+        weigh(15)
+        quant_w(14)
         product(14)
+        emit(12,2)
+        quant_w(15)
         product(15)
-        emit(12, 2)
-        emit(14, 1)
-        emit(15, 1)
+        emit(14,1)
+        emit(15,1)

@@ -48,18 +48,18 @@ def tile_rows_sigmoid_kb_kernel(tc, qT, kT, t, v, kb, out):
         q_bf = [sbuf("q_bf%d" % a, [P, hi - lo, PACK], BF16) for a, (lo, hi) in enumerate(q_spans)]
         q_codes = [sbuf("q_codes%d" % a, [P, hi - lo], U32) for a, (lo, hi) in enumerate(q_spans)]
         q_scales = [sbuf("q_scales%d" % a, [P, hi - lo], U8) for a, (lo, hi) in enumerate(q_spans)]
-        v_bf = [sbuf("v_bf%d" % a, [P, 2, E, PACK], BF16) for a in range(2)]
-        v_codes = [sbuf("v_codes%d" % a, [P, 2 * E], U32) for a in range(2)]
-        v_scales = [sbuf("v_scales%d" % a, [P, 2 * E], U8) for a in range(2)]
-        p_wide = [sbuf("p_sbw%d" % h, [P, PACK, 2 * QT], F32) for h in range(H)]
-        p_sb = [sbuf("p_sb%d" % u, [P, PACK, QT], F32)[:] for u in range(8)]
-        p_sb.extend([p_wide[u // 2][:, :, QT * (u % 2) : QT * (u % 2) + QT] for u in range(8)])
-        w_bf = [sbuf("w_bf%d" % u, [P, QT, PACK], BF16) for u in range(UNITS)]
-        w_codes = [sbuf("w_codes%d" % u, [P, QT], U32) for u in range(UNITS)]
-        w_scales = [sbuf("w_scales%d" % u, [P, QT], U8) for u in range(UNITS)]
+        v_bf = sbuf("v_bf", [P, H, E, PACK], BF16)
+        v_codes = sbuf("v_codes", [P, H * E], U32)
+        v_scales = sbuf("v_scales", [P, H * E], U8)
+        p_two = [sbuf("p_sb%d" % g, [P, PACK, 2 * QT], F32) for g in range(UNITS // 2)]
+        p_wide = p_two[H:]
+        p_sb = [p_two[u // 2][:, :, QT * (u % 2) : QT * (u % 2) + QT] for u in range(UNITS)]
+        w_bf = sbuf("w_bf", [P, UNITS * QT, PACK], BF16)
+        w_codes = sbuf("w_codes", [P, UNITS * QT], U32)
+        w_scales = sbuf("w_scales", [P, UNITS * QT], U8)
         score = [ps.tile([P, PACK, QT], F32, name="score%d" % h) for h in range(H)]
-        spare = {h: ps.tile([P, PACK, QT], F32, name="spare%d" % h) for h in (0, 2)}
-        y_bank = [ps.tile([P, H, E], F32, name="y_bank%d" % g) for g in range(2)]
+        spare = {h: ps.tile([P, PACK, QT], F32, name="spare%d" % h) for h in (0,)}
+        y_bank = [ps.tile([P, H, E], F32, name="y_bank%d" % g) for g in range(3)]
 
         def unit(u):
             if u < 8:
@@ -124,11 +124,13 @@ def tile_rows_sigmoid_kb_kernel(tc, qT, kT, t, v, kb, out):
         def quant_q(a):
             quantize(q_codes[a], q_scales[a], q_bf[a][:].rearrange("p n j -> p (n j)"))
 
-        def cast_v(eng, h):
-            cast_pairs(eng, v_bf[h // 2][:, h % 2, :, :], v_raw[h // 2][:, h % 2, :, :])
+        def cast_v(eng, h, n=1):
+            dst = v_bf[:, h : h + n, :, :].rearrange("p h (c i) r -> p h c r i", i=2)
+            src = v_raw[h // 2][:, h % 2 : h % 2 + n, :, :].rearrange("p h r (c i) -> p h c r i", i=2)
+            cast(eng, dst, src)
 
-        def quant_v(a):
-            quantize(v_codes[a], v_scales[a], v_bf[a][:].rearrange("p h e r -> p (h e r)"))
+        def quant_v():
+            quantize(v_codes, v_scales, v_bf[:].rearrange("p h e r -> p (h e r)"))
 
         def scores(units):
             for r in range(PACK):
@@ -154,32 +156,47 @@ def tile_rows_sigmoid_kb_kernel(tc, qT, kT, t, v, kb, out):
                     out=p_sb[u][:, r, :], in_=score_at(u, r), func=ACT.Sigmoid, bias=kb_sb[:, r : r + 1]
                 )
 
-        def weigh(u):
+        def weigh(u, n=1):
+            lo = QT * (u % 2)
             nc.vector.tensor_tensor(
-                out=w_bf[u][:].rearrange("p (c i) r -> p c r i", i=2),
-                in0=p_sb[u].rearrange("p r (c i) -> p c r i", i=2),
-                in1=t_sb[:].rearrange("p (c r i) -> p c r i", c=1, i=1).to_broadcast([P, QT // 2, PACK, 2]),
+                out=w_bf[:, QT * u : QT * (u + n), :].rearrange("p (c i) r -> p c r i", i=2),
+                in0=p_two[u // 2][:, :, lo : lo + n * QT].rearrange("p r (c i) -> p c r i", i=2),
+                in1=t_sb[:].rearrange("p (c r i) -> p c r i", c=1, i=1).to_broadcast([P, n * QT // 2, PACK, 2]),
                 op=ALU.mult,
             )
 
-        def quant_w(u):
-            quantize(w_codes[u], w_scales[u], w_bf[u][:].rearrange("p n r -> p (n r)"))
+        w_rows = sbuf("w_rows", [P, PACK, 2 * QT], BF16)
+
+        def weigh_rows(h):
+            for r in range(PACK):
+                nc.scalar.activation(out=w_rows[:, r, :], in_=p_wide[h][:, r, :], func=ACT.Copy, scale=t_sb[:, r : r + 1])
+
+        def weave(u):
+            lo = QT * (u % 2)
+            nc.vector.tensor_copy(
+                out=w_bf[:, QT * u : QT * (u + 1), :].rearrange("p (c i) r -> p c r i", i=4),
+                in_=w_rows[:, :, lo : lo + QT].rearrange("p r (c i) -> p c r i", i=4),
+            )
+
+        def quant_w(u, n=1):
+            cols = slice(QT * u, QT * (u + n))
+            quantize(w_codes[:, cols], w_scales[:, cols], w_bf[:, cols, :].rearrange("p n r -> p (n r)"))
 
         def y_place(u):
             if u < 14:
-                return u // H % 2, u % H
-            return u % 2, 0
+                return u // H % 3, u % H
+            return u - 13, 0
 
         def product(u):
             h = unit(u)[0]
             g, place = y_place(u)
-            ec = slice(E * (h % 2), E * (h % 2) + E)
+            ec = slice(E * h, E * h + E)
             nc.tensor.matmul_mx(
                 out=y_bank[g][:, place, :],
-                lhsT=w_codes[u][:].bitcast(FP8X4),
-                lhsT_scale=w_scales[u][:],
-                rhs=v_codes[h // 2][:, ec].bitcast(FP8X4),
-                rhs_scale=v_scales[h // 2][:, ec],
+                lhsT=w_codes[:, QT * u : QT * u + QT].bitcast(FP8X4),
+                lhsT_scale=w_scales[:, QT * u : QT * u + QT],
+                rhs=v_codes[:, ec].bitcast(FP8X4),
+                rhs_scale=v_scales[:, ec],
                 start=True,
                 stop=True,
             )
@@ -238,81 +255,67 @@ def tile_rows_sigmoid_kb_kernel(tc, qT, kT, t, v, kb, out):
         sigmoid(1)
         scores([4,5])
         weigh(1)
-        quant_w(0)
+        cast_v("v",0,2)
+        quant_w(0,2)
         sigmoid(2)
-        weigh(2)
-        quant_w(1)
         sigmoid(3)
         scores([6,7])
-        scores_wide([(0,0),(2,0)])
-        cast_v("v",0)
-        weigh(3)
-        quant_w(2)
+        scores_wide([(0,0)])
+        weigh(2,2)
+        cast_v("v",2,2)
+        quant_w(2,2)
         sigmoid(4)
-        cast_v("s",1)
-        weigh(4)
-        quant_w(3)
-        cast_v("v",2)
         sigmoid(5)
         scores_wide([(1,0),(0,1)])
-        weigh(5)
-        quant_w(4)
-        quant_v(0)
+        weigh(4,2)
+        quant_v()
+        quant_w(4,2)
         sigmoid(6)
-        cast_v("v",3)
-        weigh(6)
-        quant_w(5)
         sigmoid(7)
-        scores_wide([(3,0),(2,1)])
-        weigh(7)
-        quant_w(6)
-        quant_v(1)
+        scores_wide([(2,0),(3,0)])
+        weigh(6,2)
         sigmoid_wide(0,0)
         sigmoid_wide(1,0)
         scores_wide([(1,1)])
-        sigmoid_wide(0,1)
-        weigh(8)
-        quant_w(7)
-        weigh(9)
-        quant_w(8)
-        sigmoid_wide(3,0)
-        scores_wide([(3,1)])
         product(0)
         product(1)
         product(2)
         product(3)
+        sigmoid_wide(0,1)
+        weigh(8,2)
+        quant_w(6,2)
+        sigmoid_wide(2,0)
+        scores_wide([(2,1)])
+        sigmoid_wide(1,1)
+        sigmoid_wide(3,0)
+        scores_wide([(3,1)])
         product(4)
         product(5)
         product(6)
         product(7)
-        sigmoid_wide(1,1)
-        weigh(10)
-        quant_w(9)
-        weigh(11)
-        quant_w(10)
-        sigmoid_wide(2,0)
-        sigmoid_wide(2,1)
-        emit(0,4)
+        weigh(10,2)
+        quant_w(8,2)
+        quant_w(10,2)
         product(8)
         product(9)
         product(10)
-        weigh(12)
-        quant_w(11)
         product(11)
+        sigmoid_wide(2,1)
+        emit(0,4)
+        weigh(12,2)
         sigmoid_wide(3,1)
+        weigh_rows(3)
         emit(4,4)
-        weigh(13)
-        quant_w(12)
-        product(12)
         emit(8,4)
-        weigh(14)
-        quant_w(13)
+        weave(14)
+        quant_w(12,2)
+        product(12)
         product(13)
-        weigh(15)
+        weave(15)
         quant_w(14)
         product(14)
-        emit(12,2)
         quant_w(15)
         product(15)
+        emit(12,2)
         emit(14,1)
-        emit(15,1)
+        emit(15,1,"v")

@@ -37,10 +37,10 @@ def tile_rows_sigmoid_kb_kernel(tc, qT, kT, t, v, kb, out):
         kb_sb = sbuf("kb_sb", [P, PACK], F32)
         warm_in = sbuf("warm_in", [P, 1], F32)
         warm_out = sbuf("warm_out", [P, 1], F32)
-        k_raw = [sbuf("k_raw%d" % a, [P, PACK, NT // 2], F32) for a in range(2)]
+        k_raw = sbuf("k_raw", [P, PACK, NT], F32)
         q_spans = [(0, 128), (128, 256), (256, 512)]
         q_raw = [sbuf("q_raw%d" % a, [P, PACK, hi - lo], F32) for a, (lo, hi) in enumerate(q_spans)]
-        v_raw = [sbuf("v_raw%d" % a, [P, 2, PACK, E], F32) for a in range(2)]
+        v_raw = sbuf("v_raw", [P, H, PACK, E], F32)
 
         k_bf = [sbuf("k_bf%d" % u, [P, 2, P, PACK], BF16) for u in range(2)]
         k_codes = [sbuf("k_codes%d" % u, [P, 2 * P], U32) for u in range(2)]
@@ -51,9 +51,9 @@ def tile_rows_sigmoid_kb_kernel(tc, qT, kT, t, v, kb, out):
         v_bf = sbuf("v_bf", [P, H, E, PACK], BF16)
         v_codes = sbuf("v_codes", [P, H * E], U32)
         v_scales = sbuf("v_scales", [P, H * E], U8)
-        p_two = [sbuf("p_sb%d" % g, [P, PACK, 2 * QT], F32) for g in range(UNITS // 2)]
-        p_wide = p_two[H:]
-        p_sb = [p_two[u // 2][:, :, QT * (u % 2) : QT * (u % 2) + QT] for u in range(UNITS)]
+        p_all = [sbuf("p_sb%d" % g, [P, PACK, 4 * QT], F32) for g in range(UNITS // 4)]
+        p_wide = [p_all[2 + h // 2][:, :, 2 * QT * (h % 2) : 2 * QT * (h % 2) + 2 * QT] for h in range(H)]
+        p_sb = [p_all[u // 4][:, :, QT * (u % 4) : QT * (u % 4) + QT] for u in range(UNITS)]
         w_bf = sbuf("w_bf", [P, UNITS * QT, PACK], BF16)
         w_codes = sbuf("w_codes", [P, UNITS * QT], U32)
         w_scales = sbuf("w_scales", [P, UNITS * QT], U8)
@@ -110,9 +110,9 @@ def tile_rows_sigmoid_kb_kernel(tc, qT, kT, t, v, kb, out):
             else:
                 nc.scalar.copy(out=dst, in_=src)
 
-        def cast_k(eng, a, u):
-            dst = k_bf[u][:, :, 64 * a : 64 * a + 64, :].rearrange("p r s j -> p s j r")
-            src = k_raw[a][:].rearrange("p j (s r) -> p s j r", r=PACK)[:, :, :, 2 * u : 2 * u + 2]
+        def cast_k(eng, u, lo, hi):
+            dst = k_bf[u][:, :, lo:hi, :].rearrange("p r s j -> p s j r")
+            src = k_raw[:].rearrange("p j (s r) -> p s j r", r=PACK)[:, lo:hi, :, 2 * u : 2 * u + 2]
             cast(eng, dst, src)
 
         def cast_pairs(eng, dst, src):
@@ -126,11 +126,12 @@ def tile_rows_sigmoid_kb_kernel(tc, qT, kT, t, v, kb, out):
 
         def cast_v(eng, h, n=1):
             dst = v_bf[:, h : h + n, :, :].rearrange("p h (c i) r -> p h c r i", i=2)
-            src = v_raw[h // 2][:, h % 2 : h % 2 + n, :, :].rearrange("p h r (c i) -> p h c r i", i=2)
+            src = v_raw[:, h : h + n, :, :].rearrange("p h r (c i) -> p h c r i", i=2)
             cast(eng, dst, src)
 
-        def quant_v():
-            quantize(v_codes, v_scales, v_bf[:].rearrange("p h e r -> p (h e r)"))
+        def quant_v(h):
+            cols = slice(E * h, E * h + 2 * E)
+            quantize(v_codes[:, cols], v_scales[:, cols], v_bf[:, h : h + 2, :, :].rearrange("p h e r -> p (h e r)"))
 
         def scores(units):
             for r in range(PACK):
@@ -157,10 +158,10 @@ def tile_rows_sigmoid_kb_kernel(tc, qT, kT, t, v, kb, out):
                 )
 
         def weigh(u, n=1):
-            lo = QT * (u % 2)
+            lo = QT * (u % 4)
             nc.vector.tensor_tensor(
                 out=w_bf[:, QT * u : QT * (u + n), :].rearrange("p (c i) r -> p c r i", i=2),
-                in0=p_two[u // 2][:, :, lo : lo + n * QT].rearrange("p r (c i) -> p c r i", i=2),
+                in0=p_all[u // 4][:, :, lo : lo + n * QT].rearrange("p r (c i) -> p c r i", i=2),
                 in1=t_sb[:].rearrange("p (c r i) -> p c r i", c=1, i=1).to_broadcast([P, n * QT // 2, PACK, 2]),
                 op=ALU.mult,
             )
@@ -171,11 +172,11 @@ def tile_rows_sigmoid_kb_kernel(tc, qT, kT, t, v, kb, out):
             for r in range(PACK):
                 nc.scalar.activation(out=w_rows[:, r, :], in_=p_wide[h][:, r, :], func=ACT.Copy, scale=t_sb[:, r : r + 1])
 
-        def weave(u):
+        def weave(u, n=1):
             lo = QT * (u % 2)
             nc.vector.tensor_copy(
-                out=w_bf[:, QT * u : QT * (u + 1), :].rearrange("p (c i) r -> p c r i", i=4),
-                in_=w_rows[:, :, lo : lo + QT].rearrange("p r (c i) -> p c r i", i=4),
+                out=w_bf[:, QT * u : QT * (u + n), :].rearrange("p (c i) r -> p c r i", i=4),
+                in_=w_rows[:, :, lo : lo + n * QT].rearrange("p r (c i) -> p c r i", i=4),
             )
 
         def quant_w(u, n=1):
@@ -222,40 +223,47 @@ def tile_rows_sigmoid_kb_kernel(tc, qT, kT, t, v, kb, out):
 
         nc.scalar.dma_start(out=kb_sb[:], in_=kb.rearrange("(p r) o -> p (r o)", r=PACK))
         nc.scalar.dma_start(out=t_sb[:], in_=t.rearrange("(p r) o -> p (r o)", r=PACK))
-        for a in range(2):
-            nc.sync.dma_start(out=k_raw[a][:], in_=k_hbm[:, :, 256 * a : 256 * a + 256])
-        for a, (lo, hi) in enumerate(q_spans):
-            nc.sync.dma_start(out=q_raw[a][:], in_=q_hbm[:, :, lo:hi])
-        for a in range(2):
+        nc.sync.dma_start(out=k_raw[:], in_=k_hbm)
+        def load_q(a):
+            nc.sync.dma_start(out=q_raw[a][:], in_=q_hbm[:, :, q_spans[a][0] : q_spans[a][1]])
+
+        def load_v(h, n):
             nc.sync.dma_start(
-                out=v_raw[a][:].rearrange("p h r e -> p h (r e)"),
-                in_=v[2 * a : 2 * a + 2].rearrange("h (p r) e -> p h (r e)", r=PACK),
+                out=v_raw[:, h : h + n, :, :].rearrange("p h r e -> p h (r e)"),
+                in_=v[h : h + n].rearrange("h (p r) e -> p h (r e)", r=PACK),
             )
+
+        load_q(0)
+        load_q(1)
+        load_v(0,1)
+        load_v(1,1)
+        load_q(2)
+        load_v(2,2)
         nc.gpsimd.memset(warm_in[:], 0.0)
         nc.scalar.activation(out=warm_out[:], in_=warm_in[:], func=ACT.Sigmoid)
 
-        cast_k("v", 0, 0)
-        cast_k("v", 0, 1)
-        cast_k("v", 1, 0)
-        cast_k("s", 1, 1)
+        cast_k("v",0,0,128)
+        cast_k("s",1,40,128)
+        cast_k("v",1,0,40)
         quant_k(0)
-        cast_pairs("s", q_bf[0][:, 0:48, :], q_raw[0][:, :, 0:48])
-        cast_pairs("v", q_bf[0][:, 48:128, :], q_raw[0][:, :, 48:128])
+        cast_pairs("s", q_bf[0][:, 0:128, :], q_raw[0][:, :, 0:128])
         quant_k(1)
         quant_q(0)
         scores([0])
         scores([1, 2])
         scores([3])
         cast_pairs("s", q_bf[1][:], q_raw[1][:])
+        cast_v("v",0)
         quant_q(1)
-        cast_pairs("v", q_bf[2][:], q_raw[2][:])
+        cast_v("v",1)
+        quant_v(0)
         sigmoid(0)
         weigh(0)
-        quant_q(2)
+        cast_pairs("v", q_bf[2][:], q_raw[2][:])
         sigmoid(1)
         scores([4,5])
         weigh(1)
-        cast_v("v",0,2)
+        quant_q(2)
         quant_w(0,2)
         sigmoid(2)
         sigmoid(3)
@@ -268,7 +276,7 @@ def tile_rows_sigmoid_kb_kernel(tc, qT, kT, t, v, kb, out):
         sigmoid(5)
         scores_wide([(1,0),(0,1)])
         weigh(4,2)
-        quant_v()
+        quant_v(2)
         quant_w(4,2)
         sigmoid(6)
         sigmoid(7)

@@ -15,9 +15,25 @@ ALU = mybir.AluOpType
 
 P = 128
 PACK = 4
-ROWS = 32
+ROWS = D // PACK
 QT = 128
 UNITS = H * NQ // QT
+NARROW = 2 * H
+Q_SPANS = [(0, QT), (QT, 2 * QT), (2 * QT, NQ)]
+Y_BANKS = 3
+OUT_SCALE = 1.0 / 16.0
+
+
+def unit_place(u):
+    if u < NARROW:
+        return u % H, u // H
+    return (u - NARROW) // 2, 2 + u % 2
+
+
+def y_place(u):
+    if u < UNITS - 2:
+        return u // H % Y_BANKS, u % H
+    return u - (UNITS - 2) + 1, 0
 
 
 def tile_rows_sigmoid_kb_kernel(tc, qT, kT, t, v, kb, out):
@@ -32,200 +48,39 @@ def tile_rows_sigmoid_kb_kernel(tc, qT, kT, t, v, kb, out):
 
         q_hbm = qT.rearrange("h (p j) n -> (h p) j n", j=PACK)
         k_hbm = kT.rearrange("h (p j) n -> (h p) j n", j=PACK)
+        q_widths = [hi - lo for lo, hi in Q_SPANS]
 
         t_sb = sbuf("t_sb", [P, PACK], F32)
         kb_sb = sbuf("kb_sb", [P, PACK], F32)
         warm_in = sbuf("warm_in", [P, 1], F32)
         warm_out = sbuf("warm_out", [P, 1], F32)
         k_raw = sbuf("k_raw", [P, PACK, NT], F32)
-        q_spans = [(0, 128), (128, 256), (256, 512)]
-        q_raw = [sbuf("q_raw%d" % a, [P, PACK, hi - lo], F32) for a, (lo, hi) in enumerate(q_spans)]
+        q_raw = [sbuf("q_raw%d" % a, [P, PACK, n], F32) for a, n in enumerate(q_widths)]
         v_raw = sbuf("v_raw", [P, H, PACK, E], F32)
 
-        k_bf = [sbuf("k_bf%d" % u, [P, 2, P, PACK], BF16) for u in range(2)]
-        k_codes = [sbuf("k_codes%d" % u, [P, 2 * P], U32) for u in range(2)]
-        k_scales = [sbuf("k_scales%d" % u, [P, 2 * P], U8) for u in range(2)]
-        q_bf = [sbuf("q_bf%d" % a, [P, hi - lo, PACK], BF16) for a, (lo, hi) in enumerate(q_spans)]
-        q_codes = [sbuf("q_codes%d" % a, [P, hi - lo], U32) for a, (lo, hi) in enumerate(q_spans)]
-        q_scales = [sbuf("q_scales%d" % a, [P, hi - lo], U8) for a, (lo, hi) in enumerate(q_spans)]
+        k_bf = [sbuf("k_bf%d" % half, [P, 2, P, PACK], BF16) for half in range(2)]
+        k_codes = [sbuf("k_codes%d" % half, [P, 2 * P], U32) for half in range(2)]
+        k_scales = [sbuf("k_scales%d" % half, [P, 2 * P], U8) for half in range(2)]
+        q_bf = [sbuf("q_bf%d" % a, [P, n, PACK], BF16) for a, n in enumerate(q_widths)]
+        q_codes = [sbuf("q_codes%d" % a, [P, n], U32) for a, n in enumerate(q_widths)]
+        q_scales = [sbuf("q_scales%d" % a, [P, n], U8) for a, n in enumerate(q_widths)]
         v_bf = sbuf("v_bf", [P, H, E, PACK], BF16)
         v_codes = sbuf("v_codes", [P, H * E], U32)
         v_scales = sbuf("v_scales", [P, H * E], U8)
-        p_all = [sbuf("p_sb%d" % g, [P, PACK, 4 * QT], F32) for g in range(UNITS // 4)]
-        p_wide = [p_all[2 + h // 2][:, :, 2 * QT * (h % 2) : 2 * QT * (h % 2) + 2 * QT] for h in range(H)]
-        p_sb = [p_all[u // 4][:, :, QT * (u % 4) : QT * (u % 4) + QT] for u in range(UNITS)]
+
+        p_single = [sbuf("p_single%d" % u, [P, PACK, QT], F32) for u in range(2)]
+        p_pair = {g: sbuf("p_pair%d" % g, [P, PACK, 2 * QT], F32) for g in range(1, UNITS // 2)}
         w_bf = sbuf("w_bf", [P, UNITS * QT, PACK], BF16)
         w_codes = sbuf("w_codes", [P, UNITS * QT], U32)
         w_scales = sbuf("w_scales", [P, UNITS * QT], U8)
-        score = [ps.tile([P, PACK, QT], F32, name="score%d" % h) for h in range(H)]
-        spare = {h: ps.tile([P, PACK, QT], F32, name="spare%d" % h) for h in (0,)}
-        y_bank = [ps.tile([P, H, E], F32, name="y_bank%d" % g) for g in range(3)]
-
-        def unit(u):
-            if u < 8:
-                return u % H, u // H
-            return (u - 8) // 2, 2 + u % 2
-
-        def score_at(u, r):
-            if u == 0 and r >= 2:
-                return spare[0][:, r, :]
-            return score[u % H][:, r, :]
-
-        def wide_bank(h, half):
-            return spare[h] if h in spare and half == 0 else score[h]
-
-        def scores_wide(fills):
-            for n in range(PACK):
-                for h, half in fills:
-                    rows = slice(ROWS * h, ROWS * h + ROWS)
-                    kc = slice(P * (n // 2), P * (n // 2) + P)
-                    qcols = slice(QT * (n % 2), QT * (n % 2) + QT)
-                    nc.tensor.matmul_mx(
-                        out=wide_bank(h, half)[:, n, :],
-                        lhsT=k_codes[half][rows, kc].bitcast(FP8X4),
-                        lhsT_scale=k_scales[half][rows, kc],
-                        rhs=q_codes[2][rows, qcols].bitcast(FP8X4),
-                        rhs_scale=q_scales[2][rows, qcols],
-                        start=True,
-                        stop=True,
-                    )
-
-        def sigmoid_wide(h, half):
-            for m in range(2):
-                r = 2 * half + m
-                nc.scalar.activation(
-                    out=p_wide[h][:, r, :],
-                    in_=wide_bank(h, half)[:, 2 * m : 2 * m + 2, :].rearrange("p a n -> p (a n)"),
-                    func=ACT.Sigmoid,
-                    bias=kb_sb[:, r : r + 1],
-                )
-
-
-        def quantize(codes, scales, src):
-            nc.vector.quantize_mx(out=codes[:].bitcast(FP8X4), scales=scales[:], in_=src)
-
-        def cast(eng, dst, src):
-            if eng == "v":
-                nc.vector.tensor_copy(out=dst, in_=src)
-            else:
-                nc.scalar.copy(out=dst, in_=src)
-
-        def cast_k(eng, u, lo, hi):
-            dst = k_bf[u][:, :, lo:hi, :].rearrange("p r s j -> p s j r")
-            src = k_raw[:].rearrange("p j (s r) -> p s j r", r=PACK)[:, lo:hi, :, 2 * u : 2 * u + 2]
-            cast(eng, dst, src)
-
-        def cast_pairs(eng, dst, src):
-            cast(eng, dst.rearrange("p (c i) j -> p c j i", i=2), src.rearrange("p j (c i) -> p c j i", i=2))
-
-        def quant_k(u):
-            quantize(k_codes[u], k_scales[u], k_bf[u][:].rearrange("p r s j -> p (r s j)"))
-
-        def quant_q(a):
-            quantize(q_codes[a], q_scales[a], q_bf[a][:].rearrange("p n j -> p (n j)"))
-
-        def cast_v(eng, h, n=1):
-            dst = v_bf[:, h : h + n, :, :].rearrange("p h (c i) r -> p h c r i", i=2)
-            src = v_raw[:, h : h + n, :, :].rearrange("p h r (c i) -> p h c r i", i=2)
-            cast(eng, dst, src)
-
-        def quant_v(h):
-            cols = slice(E * h, E * h + 2 * E)
-            quantize(v_codes[:, cols], v_scales[:, cols], v_bf[:, h : h + 2, :, :].rearrange("p h e r -> p (h e r)"))
-
-        def scores(units):
-            for r in range(PACK):
-                for u in units:
-                    h, qc = u % H, u // H
-                    a = min(qc, 2)
-                    rows = slice(ROWS * h, ROWS * h + ROWS)
-                    kc = slice(P * (r % 2), P * (r % 2) + P)
-                    qcols = slice(QT * qc - q_spans[a][0], QT * qc - q_spans[a][0] + QT)
-                    nc.tensor.matmul_mx(
-                        out=score_at(u, r),
-                        lhsT=k_codes[r // 2][rows, kc].bitcast(FP8X4),
-                        lhsT_scale=k_scales[r // 2][rows, kc],
-                        rhs=q_codes[a][rows, qcols].bitcast(FP8X4),
-                        rhs_scale=q_scales[a][rows, qcols],
-                        start=True,
-                        stop=True,
-                    )
-
-        def sigmoid(u):
-            for r in range(PACK):
-                nc.scalar.activation(
-                    out=p_sb[u][:, r, :], in_=score_at(u, r), func=ACT.Sigmoid, bias=kb_sb[:, r : r + 1]
-                )
-
-        def weigh(u, n=1):
-            lo = QT * (u % 4)
-            nc.vector.tensor_tensor(
-                out=w_bf[:, QT * u : QT * (u + n), :].rearrange("p (c i) r -> p c r i", i=2),
-                in0=p_all[u // 4][:, :, lo : lo + n * QT].rearrange("p r (c i) -> p c r i", i=2),
-                in1=t_sb[:].rearrange("p (c r i) -> p c r i", c=1, i=1).to_broadcast([P, n * QT // 2, PACK, 2]),
-                op=ALU.mult,
-            )
-
         w_rows = sbuf("w_rows", [P, PACK, 2 * QT], BF16)
 
-        def weigh_rows(h):
-            for r in range(PACK):
-                nc.scalar.activation(out=w_rows[:, r, :], in_=p_wide[h][:, r, :], func=ACT.Copy, scale=t_sb[:, r : r + 1])
+        score = [ps.tile([P, PACK, QT], F32, name="score%d" % h) for h in range(H)]
+        score_extra = ps.tile([P, PACK, QT], F32, name="score_extra")
+        y_bank = [ps.tile([P, H, E], F32, name="y_bank%d" % g) for g in range(Y_BANKS)]
 
-        def weave(u, n=1):
-            lo = QT * (u % 2)
-            nc.vector.tensor_copy(
-                out=w_bf[:, QT * u : QT * (u + n), :].rearrange("p (c i) r -> p c r i", i=4),
-                in_=w_rows[:, :, lo : lo + n * QT].rearrange("p r (c i) -> p c r i", i=4),
-            )
-
-        def quant_w(u, n=1):
-            cols = slice(QT * u, QT * (u + n))
-            quantize(w_codes[:, cols], w_scales[:, cols], w_bf[:, cols, :].rearrange("p n r -> p (n r)"))
-
-        def y_place(u):
-            if u < 14:
-                return u // H % 3, u % H
-            return u - 13, 0
-
-        def product(u):
-            h = unit(u)[0]
-            g, place = y_place(u)
-            ec = slice(E * h, E * h + E)
-            nc.tensor.matmul_mx(
-                out=y_bank[g][:, place, :],
-                lhsT=w_codes[:, QT * u : QT * u + QT].bitcast(FP8X4),
-                lhsT_scale=w_scales[:, QT * u : QT * u + QT],
-                rhs=v_codes[:, ec].bitcast(FP8X4),
-                rhs_scale=v_scales[:, ec],
-                start=True,
-                stop=True,
-            )
-
-        def emit(u0, n, eng="s"):
-            g, place = y_place(u0)
-            h, qc = unit(u0)
-            y_sb = sbuf("y_sb%d" % u0, [P, n, E], F32)
-            if eng == "s":
-                nc.scalar.activation(out=y_sb[:], in_=y_bank[g][:, place : place + n, :], func=ACT.Copy, scale=1.0 / 16.0)
-            else:
-                nc.vector.tensor_scalar(out=y_sb[:], in0=y_bank[g][:, place : place + n, :], scalar1=1.0 / 16.0, scalar2=None, op0=ALU.mult)
-            if u0 < 8:
-                dst = out[h : h + n, QT * qc : QT * qc + QT, :].rearrange("h p e -> p h e")
-                nc.sync.dma_start(out=dst, in_=y_sb[:])
-            elif n == 4:
-                for a in range(2):
-                    dst = out[h + a, QT * qc : QT * (qc + 2), :].rearrange("(c p) e -> p c e", p=P)
-                    nc.sync.dma_start(out=dst, in_=y_sb[:, 2 * a : 2 * a + 2, :])
-            else:
-                dst = out[h, QT * qc : QT * (qc + n), :].rearrange("(c p) e -> p c e", p=P)
-                nc.sync.dma_start(out=dst, in_=y_sb[:])
-
-        nc.scalar.dma_start(out=kb_sb[:], in_=kb.rearrange("(p r) o -> p (r o)", r=PACK))
-        nc.scalar.dma_start(out=t_sb[:], in_=t.rearrange("(p r) o -> p (r o)", r=PACK))
-        nc.sync.dma_start(out=k_raw[:], in_=k_hbm)
         def load_q(a):
-            nc.sync.dma_start(out=q_raw[a][:], in_=q_hbm[:, :, q_spans[a][0] : q_spans[a][1]])
+            nc.sync.dma_start(out=q_raw[a][:], in_=q_hbm[:, :, Q_SPANS[a][0] : Q_SPANS[a][1]])
 
         def load_v(h, n):
             nc.sync.dma_start(
@@ -233,97 +88,236 @@ def tile_rows_sigmoid_kb_kernel(tc, qT, kT, t, v, kb, out):
                 in_=v[h : h + n].rearrange("h (p r) e -> p h (r e)", r=PACK),
             )
 
+        def cast_k(copy, half):
+            src = k_raw[:].rearrange("p j (s r) -> p s j r", r=PACK)[:, :, :, 2 * half : 2 * half + 2]
+            copy(out=k_bf[half][:].rearrange("p m s j -> p s j m"), in_=src)
+
+        def cast_q(copy, a):
+            copy(
+                out=q_bf[a][:].rearrange("p (c i) j -> p c j i", i=2),
+                in_=q_raw[a][:].rearrange("p j (c i) -> p c j i", i=2),
+            )
+
+        def cast_v(h, n):
+            nc.vector.tensor_copy(
+                out=v_bf[:, h : h + n, :, :].rearrange("p h (c i) r -> p h c r i", i=2),
+                in_=v_raw[:, h : h + n, :, :].rearrange("p h r (c i) -> p h c r i", i=2),
+            )
+
+        def quantize(codes, scales, src):
+            nc.vector.quantize_mx(out=codes.bitcast(FP8X4), scales=scales, in_=src)
+
+        def quantize_k(half):
+            quantize(k_codes[half][:], k_scales[half][:], k_bf[half][:].rearrange("p m s j -> p (m s j)"))
+
+        def quantize_q(a):
+            quantize(q_codes[a][:], q_scales[a][:], q_bf[a][:].rearrange("p n j -> p (n j)"))
+
+        def quantize_v(h, n):
+            cols = slice(E * h, E * (h + n))
+            quantize(v_codes[:, cols], v_scales[:, cols], v_bf[:, h : h + n, :, :].rearrange("p h e r -> p (h e r)"))
+
+        def quantize_w(u, n):
+            cols = slice(QT * u, QT * (u + n))
+            quantize(w_codes[:, cols], w_scales[:, cols], w_bf[:, cols, :].rearrange("p n r -> p (n r)"))
+
+        def score_matmul(dst, h, r, a, q0):
+            rows = slice(ROWS * h, ROWS * h + ROWS)
+            k_cols = slice(P * (r % 2), P * (r % 2) + P)
+            q_cols = slice(q0, q0 + QT)
+            nc.tensor.matmul_mx(
+                out=dst,
+                lhsT=k_codes[r // 2][rows, k_cols].bitcast(FP8X4),
+                lhsT_scale=k_scales[r // 2][rows, k_cols],
+                rhs=q_codes[a][rows, q_cols].bitcast(FP8X4),
+                rhs_scale=q_scales[a][rows, q_cols],
+                start=True,
+                stop=True,
+            )
+
+        def narrow_scores_at(u, r):
+            bank = score_extra if u == 0 and r >= 2 else score[u % H]
+            return bank[:, r, :]
+
+        def wide_bank(h, half):
+            return score_extra if (h, half) == (0, 0) else score[h]
+
+        def fill_narrow(units):
+            for r in range(PACK):
+                for u in units:
+                    score_matmul(narrow_scores_at(u, r), u % H, r, u // H, 0)
+
+        def fill_wide(fills):
+            for n in range(PACK):
+                for h, half in fills:
+                    score_matmul(wide_bank(h, half)[:, n, :], h, 2 * half + n // 2, 2, QT * (n % 2))
+
+        def sigmoid(dst, src, r):
+            nc.scalar.activation(out=dst, in_=src, func=ACT.Sigmoid, bias=kb_sb[:, r : r + 1])
+
+        def sigmoid_narrow(u):
+            dst = p_single[u][:] if u < 2 else p_pair[u // 2][:, :, QT * (u % 2) : QT * (u % 2) + QT]
+            for r in range(PACK):
+                sigmoid(dst[:, r, :], narrow_scores_at(u, r), r)
+
+        def sigmoid_wide(h, half):
+            for m in range(2):
+                src = wide_bank(h, half)[:, 2 * m : 2 * m + 2, :].rearrange("p a n -> p (a n)")
+                sigmoid(p_pair[NARROW // 2 + h][:, 2 * half + m, :], src, 2 * half + m)
+
+        def weigh(u, n):
+            src = p_single[u] if n == 1 else p_pair[u // 2]
+            nc.vector.tensor_tensor(
+                out=w_bf[:, QT * u : QT * (u + n), :].rearrange("p (c i) r -> p c r i", i=2),
+                in0=src[:].rearrange("p r (c i) -> p c r i", i=2),
+                in1=t_sb[:].rearrange("p (c r i) -> p c r i", c=1, i=1).to_broadcast([P, n * QT // 2, PACK, 2]),
+                op=ALU.mult,
+            )
+
+        def weigh_rows_last_pair():
+            for r in range(PACK):
+                src = p_pair[UNITS // 2 - 1][:, r, :]
+                nc.scalar.activation(out=w_rows[:, r, :], in_=src, func=ACT.Copy, scale=t_sb[:, r : r + 1])
+
+        def interleave_rows(u):
+            lo = QT * (u % 2)
+            nc.vector.tensor_copy(
+                out=w_bf[:, QT * u : QT * (u + 1), :].rearrange("p (c i) r -> p c r i", i=4),
+                in_=w_rows[:, :, lo : lo + QT].rearrange("p r (c i) -> p c r i", i=4),
+            )
+
+        def products(u0, n):
+            for u in range(u0, u0 + n):
+                bank, place = y_place(u)
+                w_cols = slice(QT * u, QT * u + QT)
+                v_cols = slice(E * unit_place(u)[0], E * unit_place(u)[0] + E)
+                nc.tensor.matmul_mx(
+                    out=y_bank[bank][:, place, :],
+                    lhsT=w_codes[:, w_cols].bitcast(FP8X4),
+                    lhsT_scale=w_scales[:, w_cols],
+                    rhs=v_codes[:, v_cols].bitcast(FP8X4),
+                    rhs_scale=v_scales[:, v_cols],
+                    start=True,
+                    stop=True,
+                )
+
+        def store(u0, y_sb, n):
+            h, tile = unit_place(u0)
+            if u0 < NARROW:
+                dst = out[h : h + n, QT * tile : QT * tile + QT, :].rearrange("h p e -> p h e")
+                nc.sync.dma_start(out=dst, in_=y_sb[:])
+                return
+            per_head = min(n, 2)
+            for a in range(n // per_head):
+                dst = out[h + a, QT * tile : QT * (tile + per_head), :].rearrange("(c p) e -> p c e", p=P)
+                nc.sync.dma_start(out=dst, in_=y_sb[:, per_head * a : per_head * (a + 1), :])
+
+        def emit(u0, n):
+            bank, place = y_place(u0)
+            y_sb = sbuf("y_sb%d" % u0, [P, n, E], F32)
+            nc.scalar.activation(out=y_sb[:], in_=y_bank[bank][:, place : place + n, :], func=ACT.Copy, scale=OUT_SCALE)
+            store(u0, y_sb, n)
+
+        def emit_last_on_vector():
+            u = UNITS - 1
+            bank, place = y_place(u)
+            y_sb = sbuf("y_sb%d" % u, [P, 1, E], F32)
+            src = y_bank[bank][:, place : place + 1, :]
+            nc.vector.tensor_scalar(out=y_sb[:], in0=src, scalar1=OUT_SCALE, scalar2=None, op0=ALU.mult)
+            store(u, y_sb, 1)
+
+        nc.scalar.dma_start(out=kb_sb[:], in_=kb.rearrange("(p r) o -> p (r o)", r=PACK))
+        nc.scalar.dma_start(out=t_sb[:], in_=t.rearrange("(p r) o -> p (r o)", r=PACK))
+        nc.sync.dma_start(out=k_raw[:], in_=k_hbm)
         load_q(0)
         load_q(1)
-        load_v(0,1)
-        load_v(1,1)
+        load_v(0, 1)
+        load_v(1, 1)
         load_q(2)
-        load_v(2,2)
+        load_v(2, 2)
         nc.gpsimd.memset(warm_in[:], 0.0)
         nc.scalar.activation(out=warm_out[:], in_=warm_in[:], func=ACT.Sigmoid)
 
-        cast_k("v",0,0,128)
-        cast_k("s",1,40,128)
-        cast_k("v",1,0,40)
-        quant_k(0)
-        cast_pairs("s", q_bf[0][:, 0:128, :], q_raw[0][:, :, 0:128])
-        quant_k(1)
-        quant_q(0)
-        scores([0])
-        scores([1, 2])
-        scores([3])
-        cast_pairs("s", q_bf[1][:], q_raw[1][:])
-        cast_v("v",0)
-        quant_q(1)
-        cast_v("v",1)
-        quant_v(0)
-        sigmoid(0)
-        weigh(0)
-        cast_pairs("v", q_bf[2][:], q_raw[2][:])
-        sigmoid(1)
-        scores([4,5])
-        weigh(1)
-        quant_q(2)
-        quant_w(0,2)
-        sigmoid(2)
-        sigmoid(3)
-        scores([6,7])
-        scores_wide([(0,0)])
-        weigh(2,2)
-        cast_v("v",2,2)
-        quant_w(2,2)
-        sigmoid(4)
-        sigmoid(5)
-        scores_wide([(1,0),(0,1)])
-        weigh(4,2)
-        quant_v(2)
-        quant_w(4,2)
-        sigmoid(6)
-        sigmoid(7)
-        scores_wide([(2,0),(3,0)])
-        weigh(6,2)
-        sigmoid_wide(0,0)
-        sigmoid_wide(1,0)
-        scores_wide([(1,1)])
-        product(0)
-        product(1)
-        product(2)
-        product(3)
-        sigmoid_wide(0,1)
-        weigh(8,2)
-        quant_w(6,2)
-        sigmoid_wide(2,0)
-        scores_wide([(2,1)])
-        sigmoid_wide(1,1)
-        sigmoid_wide(3,0)
-        scores_wide([(3,1)])
-        product(4)
-        product(5)
-        product(6)
-        product(7)
-        weigh(10,2)
-        quant_w(8,2)
-        quant_w(10,2)
-        product(8)
-        product(9)
-        product(10)
-        product(11)
-        sigmoid_wide(2,1)
-        emit(0,4)
-        weigh(12,2)
-        sigmoid_wide(3,1)
-        weigh_rows(3)
-        emit(4,4)
-        emit(8,4)
-        weave(14)
-        quant_w(12,2)
-        product(12)
-        product(13)
-        weave(15)
-        quant_w(14)
-        product(14)
-        quant_w(15)
-        product(15)
-        emit(12,2)
-        emit(14,1)
-        emit(15,1,"v")
+
+        cast_k(nc.vector.tensor_copy, 0)
+        cast_k(nc.scalar.copy, 1)
+        cast_q(nc.vector.tensor_copy, 0)
+        quantize_k(0)
+        quantize_q(0)
+        quantize_k(1)
+        fill_narrow([0])
+        fill_narrow([1, 2])
+        fill_narrow([3])
+        cast_q(nc.scalar.copy, 1)
+        cast_v(0, 1)
+        cast_v(1, 1)
+        quantize_q(1)
+        quantize_v(0, 2)
+
+        sigmoid_narrow(0)
+        weigh(0, 1)
+        cast_q(nc.vector.tensor_copy, 2)
+        sigmoid_narrow(1)
+        fill_narrow([4, 5])
+        weigh(1, 1)
+        quantize_q(2)
+        quantize_w(0, 2)
+
+        sigmoid_narrow(2)
+        sigmoid_narrow(3)
+        fill_narrow([6, 7])
+        fill_wide([(0, 0)])
+        weigh(2, 2)
+        cast_v(2, 2)
+        quantize_w(2, 2)
+
+        sigmoid_narrow(4)
+        sigmoid_narrow(5)
+        fill_wide([(1, 0), (0, 1)])
+        weigh(4, 2)
+        quantize_v(2, 2)
+        quantize_w(4, 2)
+
+        sigmoid_narrow(6)
+        sigmoid_narrow(7)
+        fill_wide([(2, 0), (3, 0)])
+        weigh(6, 2)
+
+        sigmoid_wide(0, 0)
+        sigmoid_wide(1, 0)
+        fill_wide([(1, 1)])
+        products(0, 4)
+        sigmoid_wide(0, 1)
+        weigh(8, 2)
+        quantize_w(6, 2)
+
+        sigmoid_wide(2, 0)
+        fill_wide([(2, 1)])
+        sigmoid_wide(1, 1)
+        sigmoid_wide(3, 0)
+        fill_wide([(3, 1)])
+        products(4, 4)
+        weigh(10, 2)
+        quantize_w(8, 2)
+        quantize_w(10, 2)
+        products(8, 4)
+
+        sigmoid_wide(2, 1)
+        emit(0, 4)
+        weigh(12, 2)
+
+        sigmoid_wide(3, 1)
+        weigh_rows_last_pair()
+        emit(4, 4)
+        emit(8, 4)
+        interleave_rows(14)
+        quantize_w(12, 2)
+        products(12, 2)
+        interleave_rows(15)
+        quantize_w(14, 1)
+        products(14, 1)
+        quantize_w(15, 1)
+        products(15, 1)
+        emit(12, 2)
+        emit(14, 1)
+        emit_last_on_vector()

from contextlib import ExitStack

import concourse.mybir as mybir

H, D, NQ, NT, E = 4, 128, 512, 512, 128
FLOPS = 2 * H * NT * NQ * D + 2 * H * NQ * NT * E

F32 = mybir.dt.float32
BF16 = mybir.dt.bfloat16
U32 = mybir.dt.uint32
U8 = mybir.dt.uint8
FP8X4 = mybir.dt.float8_e4m3fn_x4
ACT = mybir.ActivationFunctionType
ALU = mybir.AluOpType

P = 128
PACK = 4
ROWS = D // PACK
QT = 128
UNITS = H * NQ // QT
NARROW = 2 * H
Q_SPANS = [(0, QT), (QT, 2 * QT), (2 * QT, NQ)]
Y_BANKS = 3
OUT_SCALE = 1.0 / 16.0


def unit_place(u):
    if u < NARROW:
        return u % H, u // H
    return (u - NARROW) // 2, 2 + u % 2


def y_place(u):
    if u < UNITS - 2:
        return u // H % Y_BANKS, u % H
    return u - (UNITS - 2) + 1, 0


def tile_rows_sigmoid_kb_kernel(tc, qT, kT, t, v, kb, out):
    nc = tc.nc
    with ExitStack() as ctx:
        sb = ctx.enter_context(tc.tile_pool(name="sb", bufs=1))
        ps = ctx.enter_context(tc.psum_pool(name="ps", bufs=1))
        ctx.enter_context(tc.manual_schedule())

        def sbuf(name, shape, dtype):
            return sb.tile(shape, dtype, name=name, align_bytes=64)

        q_hbm = qT.rearrange("h (p j) n -> (h p) j n", j=PACK)
        k_hbm = kT.rearrange("h (p j) n -> (h p) j n", j=PACK)
        q_widths = [hi - lo for lo, hi in Q_SPANS]

        t_sb = sbuf("t_sb", [P, PACK], F32)
        kb_sb = sbuf("kb_sb", [P, PACK], F32)
        warm_in = sbuf("warm_in", [P, 1], F32)
        warm_out = sbuf("warm_out", [P, 1], F32)
        k_raw = sbuf("k_raw", [P, PACK, NT], F32)
        q_raw = [sbuf("q_raw%d" % a, [P, PACK, n], F32) for a, n in enumerate(q_widths)]
        v_raw = sbuf("v_raw", [P, H, PACK, E], F32)

        k_bf = [sbuf("k_bf%d" % half, [P, 2, P, PACK], BF16) for half in range(2)]
        k_codes = [sbuf("k_codes%d" % half, [P, 2 * P], U32) for half in range(2)]
        k_scales = [sbuf("k_scales%d" % half, [P, 2 * P], U8) for half in range(2)]
        q_bf = [sbuf("q_bf%d" % a, [P, n, PACK], BF16) for a, n in enumerate(q_widths)]
        q_codes = [sbuf("q_codes%d" % a, [P, n], U32) for a, n in enumerate(q_widths)]
        q_scales = [sbuf("q_scales%d" % a, [P, n], U8) for a, n in enumerate(q_widths)]
        v_bf = sbuf("v_bf", [P, H, E, PACK], BF16)
        v_codes = sbuf("v_codes", [P, H * E], U32)
        v_scales = sbuf("v_scales", [P, H * E], U8)

        p_single = [sbuf("p_single%d" % u, [P, PACK, QT], F32) for u in range(2)]
        p_pair = {g: sbuf("p_pair%d" % g, [P, PACK, 2 * QT], F32) for g in range(1, UNITS // 2)}
        w_bf = sbuf("w_bf", [P, UNITS * QT, PACK], BF16)
        w_codes = sbuf("w_codes", [P, UNITS * QT], U32)
        w_scales = sbuf("w_scales", [P, UNITS * QT], U8)
        w_rows = sbuf("w_rows", [P, PACK, 2 * QT], BF16)

        score = [ps.tile([P, PACK, QT], F32, name="score%d" % h) for h in range(H)]
        score_extra = ps.tile([P, PACK, QT], F32, name="score_extra")
        y_bank = [ps.tile([P, H, E], F32, name="y_bank%d" % g) for g in range(Y_BANKS)]

        def load_q(a):
            nc.sync.dma_start(out=q_raw[a][:], in_=q_hbm[:, :, Q_SPANS[a][0] : Q_SPANS[a][1]])

        def load_v(h, n):
            nc.sync.dma_start(
                out=v_raw[:, h : h + n, :, :].rearrange("p h r e -> p h (r e)"),
                in_=v[h : h + n].rearrange("h (p r) e -> p h (r e)", r=PACK),
            )

        def cast_k(copy, half):
            src = k_raw[:].rearrange("p j (s r) -> p s j r", r=PACK)[:, :, :, 2 * half : 2 * half + 2]
            copy(out=k_bf[half][:].rearrange("p m s j -> p s j m"), in_=src)

        def cast_q(copy, a):
            copy(
                out=q_bf[a][:].rearrange("p (c i) j -> p c j i", i=2),
                in_=q_raw[a][:].rearrange("p j (c i) -> p c j i", i=2),
            )

        def cast_v(h, n):
            nc.vector.tensor_copy(
                out=v_bf[:, h : h + n, :, :].rearrange("p h (c i) r -> p h c r i", i=2),
                in_=v_raw[:, h : h + n, :, :].rearrange("p h r (c i) -> p h c r i", i=2),
            )

        def quantize(codes, scales, src):
            nc.vector.quantize_mx(out=codes.bitcast(FP8X4), scales=scales, in_=src)

        def quantize_k(half):
            quantize(k_codes[half][:], k_scales[half][:], k_bf[half][:].rearrange("p m s j -> p (m s j)"))

        def quantize_q(a):
            quantize(q_codes[a][:], q_scales[a][:], q_bf[a][:].rearrange("p n j -> p (n j)"))

        def quantize_v(h, n):
            cols = slice(E * h, E * (h + n))
            quantize(v_codes[:, cols], v_scales[:, cols], v_bf[:, h : h + n, :, :].rearrange("p h e r -> p (h e r)"))

        def quantize_w(u, n):
            cols = slice(QT * u, QT * (u + n))
            quantize(w_codes[:, cols], w_scales[:, cols], w_bf[:, cols, :].rearrange("p n r -> p (n r)"))

        def score_matmul(dst, h, r, a, q0):
            rows = slice(ROWS * h, ROWS * h + ROWS)
            k_cols = slice(P * (r % 2), P * (r % 2) + P)
            q_cols = slice(q0, q0 + QT)
            nc.tensor.matmul_mx(
                out=dst,
                lhsT=k_codes[r // 2][rows, k_cols].bitcast(FP8X4),
                lhsT_scale=k_scales[r // 2][rows, k_cols],
                rhs=q_codes[a][rows, q_cols].bitcast(FP8X4),
                rhs_scale=q_scales[a][rows, q_cols],
                start=True,
                stop=True,
            )

        def narrow_scores_at(u, r):
            bank = score_extra if u == 0 and r >= 2 else score[u % H]
            return bank[:, r, :]

        def wide_bank(h, half):
            return score_extra if (h, half) == (0, 0) else score[h]

        def fill_narrow(units):
            for r in range(PACK):
                for u in units:
                    score_matmul(narrow_scores_at(u, r), u % H, r, u // H, 0)

        def fill_wide(fills):
            for n in range(PACK):
                for h, half in fills:
                    score_matmul(wide_bank(h, half)[:, n, :], h, 2 * half + n // 2, 2, QT * (n % 2))

        def sigmoid(dst, src, r):
            nc.scalar.activation(out=dst, in_=src, func=ACT.Sigmoid, bias=kb_sb[:, r : r + 1])

        def sigmoid_narrow(u):
            dst = p_single[u][:] if u < 2 else p_pair[u // 2][:, :, QT * (u % 2) : QT * (u % 2) + QT]
            for r in range(PACK):
                sigmoid(dst[:, r, :], narrow_scores_at(u, r), r)

        def sigmoid_wide(h, half):
            for m in range(2):
                src = wide_bank(h, half)[:, 2 * m : 2 * m + 2, :].rearrange("p a n -> p (a n)")
                sigmoid(p_pair[NARROW // 2 + h][:, 2 * half + m, :], src, 2 * half + m)

        def weigh(u, n):
            src = p_single[u] if n == 1 else p_pair[u // 2]
            nc.vector.tensor_tensor(
                out=w_bf[:, QT * u : QT * (u + n), :].rearrange("p (c i) r -> p c r i", i=2),
                in0=src[:].rearrange("p r (c i) -> p c r i", i=2),
                in1=t_sb[:].rearrange("p (c r i) -> p c r i", c=1, i=1).to_broadcast([P, n * QT // 2, PACK, 2]),
                op=ALU.mult,
            )

        def weigh_rows_last_pair():
            for r in range(PACK):
                src = p_pair[UNITS // 2 - 1][:, r, :]
                nc.scalar.activation(out=w_rows[:, r, :], in_=src, func=ACT.Copy, scale=t_sb[:, r : r + 1])

        def interleave_rows(u):
            lo = QT * (u % 2)
            nc.vector.tensor_copy(
                out=w_bf[:, QT * u : QT * (u + 1), :].rearrange("p (c i) r -> p c r i", i=4),
                in_=w_rows[:, :, lo : lo + QT].rearrange("p r (c i) -> p c r i", i=4),
            )

        def products(u0, n):
            for u in range(u0, u0 + n):
                bank, place = y_place(u)
                w_cols = slice(QT * u, QT * u + QT)
                v_cols = slice(E * unit_place(u)[0], E * unit_place(u)[0] + E)
                nc.tensor.matmul_mx(
                    out=y_bank[bank][:, place, :],
                    lhsT=w_codes[:, w_cols].bitcast(FP8X4),
                    lhsT_scale=w_scales[:, w_cols],
                    rhs=v_codes[:, v_cols].bitcast(FP8X4),
                    rhs_scale=v_scales[:, v_cols],
                    start=True,
                    stop=True,
                )

        def store(u0, y_sb, n):
            h, tile = unit_place(u0)
            if u0 < NARROW:
                dst = out[h : h + n, QT * tile : QT * tile + QT, :].rearrange("h p e -> p h e")
                nc.sync.dma_start(out=dst, in_=y_sb[:])
                return
            per_head = min(n, 2)
            for a in range(n // per_head):
                dst = out[h + a, QT * tile : QT * (tile + per_head), :].rearrange("(c p) e -> p c e", p=P)
                nc.sync.dma_start(out=dst, in_=y_sb[:, per_head * a : per_head * (a + 1), :])

        def emit(u0, n):
            bank, place = y_place(u0)
            y_sb = sbuf("y_sb%d" % u0, [P, n, E], F32)
            nc.scalar.activation(out=y_sb[:], in_=y_bank[bank][:, place : place + n, :], func=ACT.Copy, scale=OUT_SCALE)
            store(u0, y_sb, n)

        def emit_last_on_vector():
            u = UNITS - 1
            bank, place = y_place(u)
            y_sb = sbuf("y_sb%d" % u, [P, 1, E], F32)
            src = y_bank[bank][:, place : place + 1, :]
            nc.vector.tensor_scalar(out=y_sb[:], in0=src, scalar1=OUT_SCALE, scalar2=None, op0=ALU.mult)
            store(u, y_sb, 1)

        nc.scalar.dma_start(out=kb_sb[:], in_=kb.rearrange("(p r) o -> p (r o)", r=PACK))
        nc.scalar.dma_start(out=t_sb[:], in_=t.rearrange("(p r) o -> p (r o)", r=PACK))
        nc.sync.dma_start(out=k_raw[:], in_=k_hbm)
        load_q(0)
        load_q(1)
        load_v(0, 1)
        load_v(1, 1)
        load_q(2)
        load_v(2, 2)
        nc.gpsimd.memset(warm_in[:], 0.0)
        nc.scalar.activation(out=warm_out[:], in_=warm_in[:], func=ACT.Sigmoid)


        cast_k(nc.vector.tensor_copy, 0)
        cast_k(nc.scalar.copy, 1)
        cast_q(nc.vector.tensor_copy, 0)
        quantize_k(0)
        quantize_q(0)
        quantize_k(1)
        fill_narrow([0])
        fill_narrow([1, 2])
        fill_narrow([3])
        cast_q(nc.scalar.copy, 1)
        cast_v(0, 1)
        cast_v(1, 1)
        quantize_q(1)
        quantize_v(0, 2)

        sigmoid_narrow(0)
        weigh(0, 1)
        cast_q(nc.vector.tensor_copy, 2)
        sigmoid_narrow(1)
        fill_narrow([4, 5])
        weigh(1, 1)
        quantize_q(2)
        quantize_w(0, 2)

        sigmoid_narrow(2)
        sigmoid_narrow(3)
        fill_narrow([6, 7])
        fill_wide([(0, 0)])
        weigh(2, 2)
        cast_v(2, 2)
        quantize_w(2, 2)

        sigmoid_narrow(4)
        sigmoid_narrow(5)
        fill_wide([(1, 0), (0, 1)])
        weigh(4, 2)
        quantize_v(2, 2)
        quantize_w(4, 2)

        sigmoid_narrow(6)
        sigmoid_narrow(7)
        fill_wide([(2, 0), (3, 0)])
        weigh(6, 2)

        sigmoid_wide(0, 0)
        sigmoid_wide(1, 0)
        fill_wide([(1, 1)])
        products(0, 4)
        sigmoid_wide(0, 1)
        weigh(8, 2)
        quantize_w(6, 2)

        sigmoid_wide(2, 0)
        fill_wide([(2, 1)])
        sigmoid_wide(1, 1)
        sigmoid_wide(3, 0)
        fill_wide([(3, 1)])
        products(4, 4)
        weigh(10, 2)
        quantize_w(8, 2)
        quantize_w(10, 2)
        products(8, 4)

        sigmoid_wide(2, 1)
        emit(0, 4)
        weigh(12, 2)

        sigmoid_wide(3, 1)
        weigh_rows_last_pair()
        emit(4, 4)
        emit(8, 4)
        interleave_rows(14)
        quantize_w(12, 2)
        products(12, 2)
        interleave_rows(15)
        quantize_w(14, 1)
        products(14, 1)
        quantize_w(15, 1)
        products(15, 1)
        emit(12, 2)
        emit(14, 1)
        emit_last_on_vector()
